import numpy as np
import ml_dtypes


def mxq(x, axis, fmt="e4m3"):
    dtype, down = {"e4m3": (ml_dtypes.float8_e4m3fn, 7), "e5m2": (ml_dtypes.float8_e5m2, 14)}[fmt]
    v = np.moveaxis(np.asarray(x, np.float32).astype(ml_dtypes.bfloat16).astype(np.float64), axis, -1)
    blocks = v.reshape(v.shape[:-1] + (-1, 32))
    amax = np.abs(blocks).max(-1, keepdims=True)
    byte = np.maximum(np.where(amax > 0, np.frexp(amax)[1] - 1 + 127, 0) - down, 1)
    scale = np.exp2(byte - 127.0)
    codes = (blocks / scale).astype(np.float32).astype(dtype).astype(np.float64)
    return np.moveaxis((codes * scale).reshape(v.shape), -1, axis)


WIDE = False


def mx_kscale(k):
    if not WIDE:
        return np.ones(k)
    levels = np.array([10, -10, 5, -5, 0])
    if k % 512:
        return np.exp2(np.random.permutation(np.resize(levels, k // 32))).repeat(32)
    a = np.empty((k // 512, 16))
    for p in range(k // 512):
        a[p, :8] = np.random.permutation(np.resize(levels, 8))
        for g in range(8):
            far = levels[np.abs(levels - a[p, g]) >= 10]
            a[p, g + 8] = far[np.random.randint(len(far))]
    return np.exp2(a.ravel()).repeat(32)


def f64(x):
    return np.asarray(x).astype(np.float64)


def striped(idx):
    return np.tile(idx.reshape(-1, 16).T, (8, 1)).astype(np.uint16)


def unstriped(offs):
    return offs[:16].T.reshape(-1).astype(np.int64)


E2M1 = np.array([0.0, 0.5, 1.0, 1.5, 2.0, 3.0, 4.0, 6.0, -0.0, -0.5, -1.0, -1.5, -2.0, -3.0, -4.0, -6.0])


def pack_weight(w, fmt):
    k, n = w.shape
    w = f64(np.asarray(w, np.float32).astype(ml_dtypes.bfloat16)).reshape(k // 32, 32, n)
    amax = np.abs(w).max(1)
    if fmt == "e4m3":
        byte = np.frexp(amax)[1] - 1 + 127 - 7
    else:
        mant, ex = np.frexp(amax / 6.0)
        byte = np.where(mant > 0.5, ex, ex - 1) + 127
    byte = np.clip(np.where(amax > 0, byte, 1), 1, 254)
    scaled = (w * np.exp2(127.0 - byte)[:, None, :]).reshape(k, n).astype(np.float32)
    by_word = np.ascontiguousarray(scaled.reshape(k // 512, 128, 4, n).transpose(0, 1, 3, 2))
    if fmt == "e4m3":
        words = by_word.astype(ml_dtypes.float8_e4m3fn).view(np.uint8)
    else:
        c = by_word.astype(ml_dtypes.float4_e2m1fn).view(np.uint8) & 0xF
        words = (c[..., 0::2] | (c[..., 1::2] << 4)).reshape(k // 512, 128, 2 * n)
    return np.ascontiguousarray(words), np.ascontiguousarray(byte.astype(np.uint8).reshape(k // 512, 16, n))


def unpack_weight(words, scales, fmt):
    g, _, n = scales.shape
    words = np.ascontiguousarray(words).reshape(g, 128, n, -1)
    if fmt == "e4m3":
        vals = words.view(ml_dtypes.float8_e4m3fn).astype(np.float64)
    else:
        nib = np.empty((g, 128, n, 4), np.uint8)
        nib[..., 0::2] = words & 0xF
        nib[..., 1::2] = words >> 4
        vals = E2M1[nib]
    vals = vals * np.repeat(np.exp2(scales.astype(np.float64) - 127.0), 8, axis=1)[..., None]
    return vals.transpose(0, 1, 3, 2).reshape(g * 512, n)


def gelu(v):
    return 0.5 * v * (1.0 + np.tanh(np.sqrt(2.0 / np.pi) * (v + 0.044715 * v**3)))


K, H, T, S, T2, P = 1536, 512, 2048, 512, 1024, 512

def setup_inputs():
    n = np.random.standard_normal
    s = mx_kscale(K)[:, None]
    u = mx_kscale(H)[:, None]
    d = {}
    d["tab_words"], d["tab_scales"] = pack_weight(n((K, T)) * s, "e4m3")
    d["offs"] = striped(np.random.permutation(T)[:S])
    d["offs2"] = striped(np.random.permutation(T2)[:S])
    d["offs3"] = striped(np.random.permutation(T2)[:P])
    d["offs4"] = striped(np.random.permutation(T2)[:P])
    d["w1"] = (0.58 * n((K, H)) / s / K**0.5).astype(np.float32)
    d["w2_words"], d["w2_scales"] = pack_weight(0.58 * n((K, H)) / s / K**0.5, "e2m1")
    d["gain"] = (np.exp(0.3 * n(H)) * u[:, 0]).astype(np.float32)
    d["wgs"] = np.exp(0.3 * n((128, S))).astype(np.float32)
    d["page0"] = (0.6 * n((H, T2)) * u).astype(np.float32)
    d["sx"] = np.exp(0.3 * n(H)).astype(np.float32)
    d["w3"] = (1.3 * n((H, H)) / u / H**0.5).astype(np.float32)
    d["gt"] = (np.exp(0.3 * n(H)) * u[:, 0]).astype(np.float32)
    d["w4_words"], d["w4_scales"] = pack_weight(1.5 * n((H, H)) / u / H**0.5, "e4m3")
    d["rest"] = (np.exp(0.3 * n(H)) / u[:, 0]).astype(np.float32)
    return d

def reference(tab_words, tab_scales, offs, offs2, offs3, offs4, w1, w2_words, w2_scales, gain, wgs, page0, sx, w3, gt, w4_words, w4_scales, rest):
    v = unpack_weight(tab_words, tab_scales, "e4m3")[:, unstriped(offs)]
    a1 = mxq(f64(w1), 0, "e4m3").T @ v
    a2 = unpack_weight(w2_words, w2_scales, "e2m1").T @ v
    h = f64(gain)[:, None] * (np.sin(a1) + np.cos(a2))
    page = f64(page0).copy()
    page[:, unstriped(offs2)] = np.tile(f64(wgs), (H // 128, 1)) * h
    x = f64(sx)[:, None] * page[:, unstriped(offs3)]
    b = mxq(f64(w3), 0, "e4m3").T @ mxq(x, 0, "e4m3")
    z = f64(gt)[:, None] * np.tanh(b)
    y = unpack_weight(w4_words, w4_scales, "e4m3").T @ mxq(z, 0, "e4m3")
    other = f64(rest)[:, None] * page[:, unstriped(offs4)]
    return np.maximum(y, other) - b

@@ -1,0 +1,354 @@
+import math
+from contextlib import ExitStack
+
+import concourse.mybir as mybir
+from concourse.masks import make_identity
+
+K, H, T, S, T2 = 1536, 512, 2048, 512, 1024
+FLOPS = 2 * (2 * K * H * S + 2 * H * H * S)
+
+F32 = mybir.dt.float32
+BF16 = mybir.dt.bfloat16
+I32 = mybir.dt.int32
+U32 = mybir.dt.uint32
+U16 = mybir.dt.uint16
+U8 = mybir.dt.uint8
+FP8X4 = mybir.dt.float8_e4m3fn_x4
+FP4X4 = mybir.dt.float4_e2m1fn_x4
+ALU = mybir.AluOpType
+ACT = mybir.ActivationFunctionType
+
+P = 128
+PACK = 4
+PASSES = K // (P * PACK)
+QUADS = 4
+BLK = S // P
+TWO_PI = 2.0 * math.pi
+ROUNDER = 1.5 * 2.0**23
+
+
+def tile_list_tapping_panel_ledger_kernel(
+    tc, tab_words, tab_scales, offs, offs2, offs3, offs4, w1, w2_words, w2_scales, gain, wgs, page0, sx, w3, gt,
+    w4_words, w4_scales, rest, out,
+):
+    nc = tc.nc
+    with ExitStack() as ctx:
+        lists = ctx.enter_context(tc.tile_pool(name="lists", bufs=1))
+        keep = ctx.enter_context(tc.tile_pool(name="keep", bufs=1))
+        ring = ctx.enter_context(tc.tile_pool(name="ring", bufs=2))
+        psum = ctx.enter_context(tc.psum_pool(name="psum", bufs=1))
+
+        def held(name, shape, dtype, tag=None):
+            return keep.tile(shape, dtype, name=name, tag=tag or name, align_bytes=64)
+
+        def bank(number, name):
+            return psum.tile([P, S], F32, name=name, tag="bank%d" % number)
+
+        tab_s = held("tab_s", [P, PASSES * T], U8)
+        w2_s = held("w2_s", [P, PASSES * H], U8)
+        w4_s_raw = held("w4_s_raw", [P, H], U8)
+        nc.vector.memset(tab_s[:].bitcast(I32), 0)
+        nc.gpsimd.memset(w2_s[:].bitcast(I32), 0)
+        nc.gpsimd.memset(w4_s_raw[:].bitcast(I32), 0)
+        warm_in = held("warm_in", [P, 8], F32)
+        warm_out = held("warm_out", [P, 8], F32)
+        nc.gpsimd.memset(warm_in[:], 0.0)
+        nc.scalar.activation(warm_out[:], warm_in[:], ACT.Silu)
+        ident = held("ident", [P, P], F32)
+        make_identity(nc, ident[:])
+
+        def load_list(name, src):
+            tile = lists.tile([P, S // 16], U16, name=name, tag=name)
+            nc.sync.dma_start(tile[:], src)
+            return tile
+
+        def load_scale_rows(plane, src, quads):
+            passes = src.shape[0]
+            for q in quads:
+                nc.sync.dma_start(
+                    out=plane[32 * q : 32 * q + 4, :].bitcast(I32).rearrange("r (a n) -> r a n", a=passes),
+                    in_=src[:, 4 * q : 4 * q + 4, :].bitcast(I32).rearrange("a r n -> r a n"),
+                )
+
+        def load_tab(a):
+            tile = held("tab_w%d" % a, [P, T], I32)
+            nc.sync.dma_start(out=tile[:], in_=tab_words[a].rearrange("p n i -> p (n i)").bitcast(I32))
+            return tile
+
+        def load_rows(name, src):
+            tile = held(name, [P, PACK, src.shape[1]], F32)
+            nc.sync.dma_start(out=tile[:], in_=src.rearrange("(p j) c -> p j c", j=PACK))
+            return tile
+
+        def load_vector(name, src):
+            tile = held(name, [P, PACK], F32)
+            nc.sync.dma_start(out=tile[:], in_=src.rearrange("(p t) -> p t", t=PACK))
+            return tile
+
+        def load_page(t):
+            tile = held("page%d" % t, [P, T2], F32)
+            nc.sync.dma_start(out=tile[:], in_=page0.rearrange("(p t) c -> t p c", t=PACK)[t])
+            return tile
+
+        idx = load_list("idx", offs)
+        tab_w = [load_tab(0)]
+        load_scale_rows(tab_s, tab_scales, range(QUADS))
+        tab_w.append(load_tab(1))
+        w2_w = held("w2_w", [P, PASSES * 2 * H], U8)
+        nc.sync.dma_start(
+            out=w2_w[:].bitcast(I32).rearrange("p (a n) -> p a n", a=PASSES),
+            in_=w2_words.bitcast(I32).rearrange("a p n -> p a n"),
+        )
+        load_scale_rows(w2_s, w2_scales, range(QUADS))
+        tab_w.append(load_tab(2))
+        w1_raw = [load_rows("w1_raw0", w1[0:512, :])]
+        load_scale_rows(w4_s_raw, w4_scales, range(0, 2))
+        w1_raw.append(load_rows("w1_raw1", w1[512:1024, :]))
+        load_scale_rows(w4_s_raw, w4_scales, range(2, 4))
+        gain_t = load_vector("gain_t", gain)
+        w1_last = [load_rows("w1_last%d" % c, w1[1024:1536, 256 * c : 256 * (c + 1)]) for c in range(2)]
+        idx2 = load_list("idx2", offs2)
+        w4_w_raw = held("w4_w_raw", [P, H], I32)
+        nc.sync.dma_start(out=w4_w_raw[:], in_=w4_words[0].rearrange("p n i -> p (n i)").bitcast(I32))
+        page = [load_page(0)]
+        wgs_t = held("wgs_t", [P, PACK * S], F32)
+        for q in range(QUADS):
+            nc.sync.dma_start(out=wgs_t[32 * q : 32 * (q + 1), :], in_=wgs.rearrange("(p t) j -> p (t j)", t=PACK))
+        sx_t = load_vector("sx_t", sx)
+        idx3 = load_list("idx3", offs3)
+        page.append(load_page(1))
+        w3_raw = load_rows("w3_raw", w3)
+        idx4 = load_list("idx4", offs4)
+        rest_t = load_vector("rest_t", rest)
+        gt_t = load_vector("gt_t", gt)
+        page.append(load_page(2))
+        page.append(load_page(3))
+
+        v_w, v_s = [], []
+        for a in range(PASSES):
+            scales = held("v_s%d" % a, [P, S], U8)
+            nc.vector.tensor_copy(scales[:], tab_s[:, a * T : (a + 1) * T].indirect(idx[:]))
+            v_s.append(scales)
+            words = held("v_w%d" % a, [P, S], U32)
+            nc.vector.tensor_copy(words[:], tab_w[a][:].bitcast(U32).indirect(idx[:]))
+            v_w.append(words)
+
+        a2 = [bank(u, "a2_%d" % u) for u in range(BLK)]
+        for a in range(PASSES):
+            for u in range(BLK):
+                toks = slice(u * P, (u + 1) * P)
+                nc.tensor.matmul_mx(
+                    out=a2[u][:],
+                    lhsT=v_w[a][:, toks].bitcast(FP8X4),
+                    lhsT_scale=v_s[a][:, toks],
+                    rhs=w2_w[:, a * 2 * H : (a + 1) * 2 * H].bitcast(FP4X4),
+                    rhs_scale=w2_s[:, a * H : (a + 1) * H],
+                    start=(a == 0),
+                    stop=(a == PASSES - 1),
+                )
+        def sine_vector(result, acc, quarter_turns):
+            turns = ring.tile([P, PACK, P], I32, name="turns_v")
+            nc.vector.tensor_scalar(turns[:], acc, 1.0 / TWO_PI, 0.25 * quarter_turns, ALU.mult, ALU.add)
+            rem = ring.tile([P, PACK, P], F32, name="rem")
+            nc.vector.scalar_tensor_tensor(rem[:], turns[:], -TWO_PI, acc, ALU.mult, ALU.add)
+            nc.scalar.activation(result, rem[:], ACT.Sin, bias=quarter_turns * math.pi / 2)
+
+        def sine_scalar(result, acc, quarter_turns, frac):
+            nc.scalar.activation(frac, acc, ACT.Copy, scale=1.0 / TWO_PI, bias=0.25 * quarter_turns)
+            turns = ring.tile([P, PACK, P], U32, name="turns_s")
+            nc.scalar.activation(turns[:], frac, ACT.Copy, bias=ROUNDER)
+            rem = ring.tile([P, PACK, P], F32, name="rem")
+            nc.vector.scalar_tensor_tensor(
+                rem[:], turns[:].bitcast(I32), ROUNDER, frac, ALU.subtract, ALU.subtract
+            )
+            nc.scalar.activation(result, rem[:], ACT.Sin, scale=-TWO_PI)
+
+        cos_all = held("cos_all", [P, BLK, PACK, P], F32, tag="w1_raw0")
+        cos2 = [cos_all[:, u] for u in range(BLK)]
+        for u in range(2):
+            sine_vector(cos2[u], a2[u][:].rearrange("p (m t) -> p t m", t=PACK), 1)
+
+        def deal_and_round(copy, grouped, raw, m0):
+            count = raw.shape[2] // PACK
+            copy(
+                grouped[:].rearrange("p (t m j) -> p m j t", t=PACK, j=PACK)[:, m0 : m0 + count],
+                raw[:].rearrange("p j (m t) -> p m j t", t=PACK),
+            )
+
+        def quantise(codes, scales, grouped, c0, count):
+            nc.vector.quantize_mx(
+                out=codes[:, c0 : c0 + count].bitcast(FP8X4),
+                scales=scales[:, c0 : c0 + count],
+                in_=grouped[:, PACK * c0 : PACK * (c0 + count)],
+            )
+
+        w1_w = [held("w1_w%d" % a, [P, H], U32) for a in range(PASSES)]
+        w1_s = [held("w1_s%d" % a, [P, H], U8) for a in range(PASSES)]
+        for a in range(PASSES - 1):
+            grouped = held("w1_bf%d" % a, [P, PACK * H], BF16)
+            deal_and_round(nc.scalar.copy if a == 0 else nc.vector.tensor_copy, grouped, w1_raw[a], 0)
+            quantise(w1_w[a], w1_s[a], grouped, 0, H)
+        grouped = held("w1_bf2", [P, PACK * H], BF16)
+        for c in range(2):
+            deal_and_round(nc.vector.tensor_copy, grouped, w1_last[c], 64 * c)
+        for t in range(PACK):
+            quantise(w1_w[2], w1_s[2], grouped, t * P, P)
+
+        a1 = [bank(4 + t, "a1_%d" % t) for t in range(PACK)]
+        for a in range(PASSES):
+            for t in range(PACK):
+                for u in range(BLK):
+                    toks = slice(u * P, (u + 1) * P)
+                    nc.tensor.matmul_mx(
+                        out=a1[t][:, toks],
+                        lhsT=v_w[a][:, toks].bitcast(FP8X4),
+                        lhsT_scale=v_s[a][:, toks],
+                        rhs=w1_w[a][:, t * P : (t + 1) * P].bitcast(FP8X4),
+                        rhs_scale=w1_s[a][:, t * P : (t + 1) * P],
+                        start=(a == 0 and u == 0),
+                        stop=(a == PASSES - 1 and u == BLK - 1),
+                    )
+
+        frac2 = held("frac2", [P, 2, PACK, P], F32, tag="w1_bf0")
+        for u in range(2, BLK):
+            sine_scalar(cos2[u], a2[u][:].rearrange("p (m t) -> p t m", t=PACK), 1, frac2[:, u - 2])
+
+        h = []
+        for t in range(PACK):
+            total = bank(t, "total%d" % t)
+            for u in range(BLK):
+                nc.tensor.matmul(
+                    total[:, u * P : (u + 1) * P], lhsT=cos2[u][:, t, :], rhs=ident[:],
+                    start=(u == 0), stop=False, is_transpose=True,
+                )
+            sin1 = ring.tile([P, BLK, P], F32, name="sin1")
+            acc = a1[t][:].rearrange("p (u m) -> p u m", u=BLK)
+            if t == 0:
+                sine_vector(sin1[:], acc, 0)
+            else:
+                frac1 = ring.tile([P, BLK, P], F32, name="frac1")
+                sine_scalar(sin1[:], acc, 0, frac1[:])
+            for u in range(BLK):
+                nc.tensor.matmul(
+                    total[:, u * P : (u + 1) * P], lhsT=sin1[:, u, :], rhs=ident[:],
+                    start=False, stop=(u == BLK - 1), is_transpose=True,
+                )
+            h.append(held("h%d" % t, [P, S], F32))
+            nc.scalar.activation(h[t][:], total[:], ACT.Copy, scale=gain_t[:, t : t + 1])
+        w4_w = held("w4_w", [P, H], I32)
+        nc.vector.tensor_copy(
+            w4_w[:].rearrange("p (t m) -> p m t", t=PACK), w4_w_raw[:].rearrange("p (m t) -> p m t", t=PACK)
+        )
+        w4_s = held("w4_s", [P, H], U8)
+        nc.vector.tensor_copy(
+            w4_s[:].rearrange("p (t m) -> p m t", t=PACK), w4_s_raw[:].rearrange("p (m t) -> p m t", t=PACK)
+        )
+
+        w3_bf = held("w3_bf", [P, PACK * H], BF16)
+        deal_and_round(nc.scalar.copy, w3_bf, w3_raw, 0)
+
+
+        x_bf = [held("x_bf%d" % c, [P, 256 * PACK], BF16) for c in range(2)]
+        other = held("other", [P, PACK, S], F32)
+        rested = {}
+
+        def gather_rested(t, tag):
+            rested[t] = held("rested%d" % t, [P, S], F32, tag=tag)
+            nc.vector.tensor_copy(rested[t][:], page[t][:].indirect(idx4[:]))
+
+        def scale_rested(t):
+            nc.scalar.activation(other[:, t, :], rested[t][:], ACT.Copy, scale=rest_t[:, t : t + 1])
+
+        for t in range(PACK):
+            nc.vector.tensor_tensor(page[t][:].indirect(idx2[:]), h[t][:], wgs_t[:, t * S : (t + 1) * S], ALU.mult)
+            due = held("due%d" % t, [P, S], F32)
+            pieces = 1 if t < PACK - 1 else 2
+            width = S // pieces
+            for c in range(pieces):
+                nc.vector.tensor_copy(
+                    due[:, c * width : (c + 1) * width],
+                    page[t][:].indirect(idx3[:, c * width // 16 : (c + 1) * width // 16]),
+                )
+            width = 256 if t < PACK - 1 else P
+            for c0 in range(0, S, width):
+                lanes = x_bf[c0 // 256][:].rearrange("p (j t) -> p t j", t=PACK)
+                nc.scalar.activation(
+                    lanes[:, t, c0 % 256 : c0 % 256 + width],
+                    due[:, c0 : c0 + width],
+                    ACT.Copy,
+                    scale=sx_t[:, t : t + 1],
+                )
+            if t == 2:
+                w3_w = held("w3_w", [P, H], U32, tag="h2")
+                w3_s = held("w3_s", [P, H], U8)
+                quantise(w3_w, w3_s, w3_bf, 0, H)
+            if t < 2:
+                gather_rested(t, None)
+                scale_rested(t)
+
+        gather_rested(3, None)
+
+        b = []
+        for q in range(BLK):
+            x_w = held("x_w%d" % q, [P, P], U32)
+            x_s = held("x_s%d" % q, [P, P], U8)
+            c0 = (q % 2) * P * PACK
+            nc.vector.quantize_mx(
+                out=x_w[:].bitcast(FP8X4), scales=x_s[:], in_=x_bf[q // 2][:, c0 : c0 + P * PACK]
+            )
+            acc = bank(4 + q, "b%d" % q)
+            for t in range(PACK):
+                cols = slice(t * P, (t + 1) * P)
+                nc.tensor.matmul_mx(
+                    out=acc[:, cols],
+                    lhsT=w3_w[:, cols].bitcast(FP8X4),
+                    lhsT_scale=w3_s[:, cols],
+                    rhs=x_w[:].bitcast(FP8X4),
+                    rhs_scale=x_s[:],
+                    start=True,
+                    stop=True,
+                )
+            b.append(acc)
+        gather_rested(2, "x_bf1")
+
+        y = []
+        for q in range(BLK):
+            th = ring.tile([P, S], F32, name="th")
+            nc.scalar.activation(th[:], b[q][:], ACT.Tanh)
+            z_rows = ring.tile([P, S], BF16, name="z_rows")
+            for t in range(PACK):
+                cols = slice(t * P, (t + 1) * P)
+                nc.scalar.activation(z_rows[:, cols], th[:, cols], ACT.Copy, scale=gt_t[:, t : t + 1])
+            z_bf = ring.tile([P, S], BF16, name="z_bf", align_bytes=64)
+            nc.vector.tensor_copy(
+                z_bf[:].rearrange("p (c i t) -> p c t i", i=4, t=PACK),
+                z_rows[:].rearrange("p (t c i) -> p c t i", i=4, t=PACK),
+            )
+            z_w = ring.tile([P, P], U32, name="z_w", align_bytes=64)
+            z_s = ring.tile([P, P], U8, name="z_s", align_bytes=64)
+            nc.vector.quantize_mx(out=z_w[:].bitcast(FP8X4), scales=z_s[:], in_=z_bf[:])
+            acc = bank(q, "y%d" % q)
+            for t in range(PACK):
+                cols = slice(t * P, (t + 1) * P)
+                nc.tensor.matmul_mx(
+                    out=acc[:, cols],
+                    lhsT=w4_w[:, cols].bitcast(FP8X4),
+                    lhsT_scale=w4_s[:, cols],
+                    rhs=z_w[:].bitcast(FP8X4),
+                    rhs_scale=z_s[:],
+                    start=True,
+                    stop=True,
+                )
+            y.append(acc)
+            if q < 2:
+                scale_rested(3 - q)
+
+        out_rows = out.rearrange("(p t) j -> p t j", t=PACK)
+        for q in range(BLK):
+            best = ring.tile([P, PACK, P], F32, name="best")
+            nc.vector.tensor_tensor(
+                best[:], y[q][:].rearrange("p (t j) -> p t j", t=PACK), other[:, :, q * P : (q + 1) * P], ALU.max
+            )
+            res = held("res%d" % q, [P, PACK, P], F32)
+            nc.vector.tensor_tensor(res[:], best[:], b[q][:].rearrange("p (t j) -> p t j", t=PACK), ALU.subtract)
+            nc.sync.dma_start(out=out_rows[:, :, q * P : (q + 1) * P], in_=res[:])

@@ -62,12 +62,12 @@ def tile_list_tapping_panel_ledger_kernel(
             nc.sync.dma_start(tile[:], src)
             return tile
 
-        def load_scale_rows(plane, src, quads):
+        def load_scale_rows(plane, src):
             passes = src.shape[0]
-            for q in quads:
+            for r in range(4):
                 nc.sync.dma_start(
-                    out=plane[32 * q : 32 * q + 4, :].bitcast(I32).rearrange("r (a n) -> r a n", a=passes),
-                    in_=src[:, 4 * q : 4 * q + 4, :].bitcast(I32).rearrange("a r n -> r a n"),
+                    out=plane[r:P:32, :].bitcast(I32).rearrange("q (a n) -> q a n", a=passes),
+                    in_=src[:, r:16:4, :].bitcast(I32).rearrange("a q n -> q a n"),
                 )
 
         def load_tab(a):
@@ -92,27 +92,26 @@ def tile_list_tapping_panel_ledger_kernel(
 
         idx = load_list("idx", offs)
         tab_w = [load_tab(0)]
-        load_scale_rows(tab_s, tab_scales, range(QUADS))
+        load_scale_rows(tab_s, tab_scales)
         tab_w.append(load_tab(1))
         w2_w = held("w2_w", [P, PASSES * 2 * H], U8)
         nc.sync.dma_start(
             out=w2_w[:].bitcast(I32).rearrange("p (a n) -> p a n", a=PASSES),
             in_=w2_words.bitcast(I32).rearrange("a p n -> p a n"),
         )
-        load_scale_rows(w2_s, w2_scales, range(QUADS))
+        load_scale_rows(w2_s, w2_scales)
         tab_w.append(load_tab(2))
         w1_raw = [load_rows("w1_raw0", w1[0:512, :])]
-        load_scale_rows(w4_s_raw, w4_scales, range(0, 2))
         w1_raw.append(load_rows("w1_raw1", w1[512:1024, :]))
-        load_scale_rows(w4_s_raw, w4_scales, range(2, 4))
-        gain_t = load_vector("gain_t", gain)
         w1_last = [load_rows("w1_last%d" % c, w1[1024:1536, 256 * c : 256 * (c + 1)]) for c in range(2)]
-        idx2 = load_list("idx2", offs2)
         w4_w_raw = held("w4_w_raw", [P, H], I32)
         nc.sync.dma_start(out=w4_w_raw[:], in_=w4_words[0].rearrange("p n i -> p (n i)").bitcast(I32))
+        gain_t = load_vector("gain_t", gain)
+        idx2 = load_list("idx2", offs2)
         page = [load_page(0)]
+        load_scale_rows(w4_s_raw, w4_scales)
         wgs_t = held("wgs_t", [P, PACK * S], F32)
-        for q in range(QUADS):
+        for q in (0, 2, 1, 3):
             nc.sync.dma_start(out=wgs_t[32 * q : 32 * (q + 1), :], in_=wgs.rearrange("(p t) j -> p (t j)", t=PACK))
         sx_t = load_vector("sx_t", sx)
         idx3 = load_list("idx3", offs3)
@@ -146,10 +145,9 @@ def tile_list_tapping_panel_ledger_kernel(
                     start=(a == 0),
                     stop=(a == PASSES - 1),
                 )
-        def sine_vector(result, acc, quarter_turns):
+        def sine_vector(result, acc, quarter_turns, rem):
             turns = ring.tile([P, PACK, P], I32, name="turns_v")
             nc.vector.tensor_scalar(turns[:], acc, 1.0 / TWO_PI, 0.25 * quarter_turns, ALU.mult, ALU.add)
-            rem = ring.tile([P, PACK, P], F32, name="rem")
             nc.vector.scalar_tensor_tensor(rem[:], turns[:], -TWO_PI, acc, ALU.mult, ALU.add)
             nc.scalar.activation(result, rem[:], ACT.Sin, bias=quarter_turns * math.pi / 2)
 
@@ -166,7 +164,8 @@ def tile_list_tapping_panel_ledger_kernel(
         cos_all = held("cos_all", [P, BLK, PACK, P], F32, tag="w1_raw0")
         cos2 = [cos_all[:, u] for u in range(BLK)]
         for u in range(2):
-            sine_vector(cos2[u], a2[u][:].rearrange("p (m t) -> p t m", t=PACK), 1)
+            rem2 = ring.tile([P, PACK, P], F32, name="rem")
+            sine_vector(cos2[u], a2[u][:].rearrange("p (m t) -> p t m", t=PACK), 1, rem2)
 
         def deal_and_round(copy, grouped, raw, m0):
             count = raw.shape[2] // PACK
@@ -190,24 +189,33 @@ def tile_list_tapping_panel_ledger_kernel(
             quantise(w1_w[a], w1_s[a], grouped, 0, H)
         grouped = held("w1_bf2", [P, PACK * H], BF16)
         for c in range(2):
-            deal_and_round(nc.vector.tensor_copy, grouped, w1_last[c], 64 * c)
+            deal_and_round(nc.scalar.copy if c == 0 else nc.vector.tensor_copy, grouped, w1_last[c], 64 * c)
         for t in range(PACK):
             quantise(w1_w[2], w1_s[2], grouped, t * P, P)
 
         a1 = [bank(4 + t, "a1_%d" % t) for t in range(PACK)]
         for a in range(PASSES):
-            for t in range(PACK):
-                for u in range(BLK):
-                    toks = slice(u * P, (u + 1) * P)
-                    nc.tensor.matmul_mx(
-                        out=a1[t][:, toks],
-                        lhsT=v_w[a][:, toks].bitcast(FP8X4),
-                        lhsT_scale=v_s[a][:, toks],
-                        rhs=w1_w[a][:, t * P : (t + 1) * P].bitcast(FP8X4),
-                        rhs_scale=w1_s[a][:, t * P : (t + 1) * P],
-                        start=(a == 0 and u == 0),
-                        stop=(a == PASSES - 1 and u == BLK - 1),
-                    )
+            for u in range(BLK):
+                toks = slice(u * P, (u + 1) * P)
+                nc.tensor.matmul_mx(
+                    out=a1[0][:, toks],
+                    lhsT=v_w[a][:, toks].bitcast(FP8X4),
+                    lhsT_scale=v_s[a][:, toks],
+                    rhs=w1_w[a][:, 0:P].bitcast(FP8X4),
+                    rhs_scale=w1_s[a][:, 0:P],
+                    start=(a == 0 and u == 0),
+                    stop=(a == PASSES - 1 and u == BLK - 1),
+                )
+            for t in range(1, PACK):
+                nc.tensor.matmul_mx(
+                    out=a1[t][:],
+                    lhsT=w1_w[a][:, t * P : (t + 1) * P].bitcast(FP8X4),
+                    lhsT_scale=w1_s[a][:, t * P : (t + 1) * P],
+                    rhs=v_w[a][:].bitcast(FP8X4),
+                    rhs_scale=v_s[a][:],
+                    start=(a == 0),
+                    stop=(a == PASSES - 1),
+                )
 
         frac2 = held("frac2", [P, 2, PACK, P], F32, tag="w1_bf0")
         for u in range(2, BLK):
@@ -222,12 +230,26 @@ def tile_list_tapping_panel_ledger_kernel(
                     start=(u == 0), stop=False, is_transpose=True,
                 )
             sin1 = ring.tile([P, BLK, P], F32, name="sin1")
-            acc = a1[t][:].rearrange("p (u m) -> p u m", u=BLK)
             if t == 0:
-                sine_vector(sin1[:], acc, 0)
+                rem0 = held("rem0", [P, BLK, P], F32, tag="frac1")
+                sine_vector(sin1[:], a1[0][:].rearrange("p (u m) -> p u m", u=BLK), 0, rem0)
             else:
-                frac1 = ring.tile([P, BLK, P], F32, name="frac1")
-                sine_scalar(sin1[:], acc, 0, frac1[:])
+                frac1 = held("frac1_%d" % t, [P, S], F32, tag="frac1")
+                nc.scalar.activation(frac1[:], a1[t][:], ACT.Copy, scale=1.0 / TWO_PI)
+                turns1 = ring.tile([P, S], U32, name="turns1")
+                nc.scalar.activation(turns1[:], frac1[:], ACT.Copy, bias=ROUNDER)
+                back1 = ring.tile([P, S], F32, name="back1")
+                nc.scalar.activation(back1[:], turns1[:], ACT.Copy, scale=-1.0, bias=ROUNDER)
+                rem1 = bank(4 + t, "rem1_%d" % t)
+                for i, part in enumerate((frac1, back1)):
+                    for u in range(BLK):
+                        nc.tensor.matmul(
+                            rem1[:, u * P : (u + 1) * P], lhsT=part[:, u * P : (u + 1) * P], rhs=ident[:],
+                            start=(i == 0 and u == 0), stop=(i == 1 and u == BLK - 1), is_transpose=True,
+                        )
+                nc.scalar.activation(
+                    sin1[:], rem1[:].rearrange("p (u m) -> p u m", u=BLK), ACT.Sin, scale=TWO_PI
+                )
             for u in range(BLK):
                 nc.tensor.matmul(
                     total[:, u * P : (u + 1) * P], lhsT=sin1[:, u, :], rhs=ident[:],

@@ -85,6 +85,13 @@ def tile_list_tapping_panel_ledger_kernel(
             nc.sync.dma_start(out=tile[:], in_=src.rearrange("(p t) -> p t", t=PACK))
             return tile
 
+        def load_wgs(name, t0, t1):
+            tile = held(name, [P, (t1 - t0) * S], F32)
+            rows = wgs.rearrange("(p t) j -> p (t j)", t=PACK)[:, t0 * S : t1 * S]
+            for q in (0, 2, 1, 3):
+                nc.sync.dma_start(out=tile[32 * q : 32 * (q + 1), :], in_=rows)
+            return tile
+
         def load_page(t):
             tile = held("page%d" % t, [P, T2], F32)
             nc.sync.dma_start(out=tile[:], in_=page0.rearrange("(p t) c -> t p c", t=PACK)[t])
@@ -104,15 +111,15 @@ def tile_list_tapping_panel_ledger_kernel(
         w1_raw = [load_rows("w1_raw0", w1[0:512, :])]
         w1_raw.append(load_rows("w1_raw1", w1[512:1024, :]))
         w1_last = [load_rows("w1_last%d" % c, w1[1024:1536, 256 * c : 256 * (c + 1)]) for c in range(2)]
-        w4_w_raw = held("w4_w_raw", [P, H], I32)
-        nc.sync.dma_start(out=w4_w_raw[:], in_=w4_words[0].rearrange("p n i -> p (n i)").bitcast(I32))
         gain_t = load_vector("gain_t", gain)
         idx2 = load_list("idx2", offs2)
         page = [load_page(0)]
+        wgs_first = load_wgs("wgs_first", 0, 1)
+        w4_w_raw = held("w4_w_raw", [P, H], I32)
+        nc.sync.dma_start(out=w4_w_raw[:], in_=w4_words[0].rearrange("p n i -> p (n i)").bitcast(I32))
         load_scale_rows(w4_s_raw, w4_scales)
-        wgs_t = held("wgs_t", [P, PACK * S], F32)
-        for q in (0, 2, 1, 3):
-            nc.sync.dma_start(out=wgs_t[32 * q : 32 * (q + 1), :], in_=wgs.rearrange("(p t) j -> p (t j)", t=PACK))
+        wgs_later = load_wgs("wgs_later", 1, PACK)
+        wgs_t = [wgs_first[:]] + [wgs_later[:, i * S : (i + 1) * S] for i in range(PACK - 1)]
         sx_t = load_vector("sx_t", sx)
         idx3 = load_list("idx3", offs3)
         page.append(load_page(1))
@@ -125,12 +132,12 @@ def tile_list_tapping_panel_ledger_kernel(
 
         v_w, v_s = [], []
         for a in range(PASSES):
-            scales = held("v_s%d" % a, [P, S], U8)
-            nc.vector.tensor_copy(scales[:], tab_s[:, a * T : (a + 1) * T].indirect(idx[:]))
-            v_s.append(scales)
             words = held("v_w%d" % a, [P, S], U32)
             nc.vector.tensor_copy(words[:], tab_w[a][:].bitcast(U32).indirect(idx[:]))
             v_w.append(words)
+            scales = held("v_s%d" % a, [P, S], U8)
+            nc.vector.tensor_copy(scales[:], tab_s[:, a * T : (a + 1) * T].indirect(idx[:]))
+            v_s.append(scales)
 
         a2 = [bank(u, "a2_%d" % u) for u in range(BLK)]
         for a in range(PASSES):
@@ -155,16 +162,16 @@ def tile_list_tapping_panel_ledger_kernel(
             nc.scalar.activation(frac, acc, ACT.Copy, scale=1.0 / TWO_PI, bias=0.25 * quarter_turns)
             turns = ring.tile([P, PACK, P], U32, name="turns_s")
             nc.scalar.activation(turns[:], frac, ACT.Copy, bias=ROUNDER)
-            rem = ring.tile([P, PACK, P], F32, name="rem")
+            rem = ring.tile([P, PACK, P], F32, name="rem", bufs=BLK)
             nc.vector.scalar_tensor_tensor(
                 rem[:], turns[:].bitcast(I32), ROUNDER, frac, ALU.subtract, ALU.subtract
             )
             nc.scalar.activation(result, rem[:], ACT.Sin, scale=-TWO_PI)
 
-        cos_all = held("cos_all", [P, BLK, PACK, P], F32, tag="w1_raw0")
+        cos_all = held("cos_all", [P, BLK, PACK, P], F32, tag="w1_last0")
         cos2 = [cos_all[:, u] for u in range(BLK)]
         for u in range(2):
-            rem2 = ring.tile([P, PACK, P], F32, name="rem")
+            rem2 = ring.tile([P, PACK, P], F32, name="rem", bufs=BLK)
             sine_vector(cos2[u], a2[u][:].rearrange("p (m t) -> p t m", t=PACK), 1, rem2)
 
         def deal_and_round(copy, grouped, raw, m0):
@@ -195,18 +202,7 @@ def tile_list_tapping_panel_ledger_kernel(
 
         a1 = [bank(4 + t, "a1_%d" % t) for t in range(PACK)]
         for a in range(PASSES):
-            for u in range(BLK):
-                toks = slice(u * P, (u + 1) * P)
-                nc.tensor.matmul_mx(
-                    out=a1[0][:, toks],
-                    lhsT=v_w[a][:, toks].bitcast(FP8X4),
-                    lhsT_scale=v_s[a][:, toks],
-                    rhs=w1_w[a][:, 0:P].bitcast(FP8X4),
-                    rhs_scale=w1_s[a][:, 0:P],
-                    start=(a == 0 and u == 0),
-                    stop=(a == PASSES - 1 and u == BLK - 1),
-                )
-            for t in range(1, PACK):
+            for t in range(PACK):
                 nc.tensor.matmul_mx(
                     out=a1[t][:],
                     lhsT=w1_w[a][:, t * P : (t + 1) * P].bitcast(FP8X4),
@@ -217,7 +213,7 @@ def tile_list_tapping_panel_ledger_kernel(
                     stop=(a == PASSES - 1),
                 )
 
-        frac2 = held("frac2", [P, 2, PACK, P], F32, tag="w1_bf0")
+        frac2 = held("frac2", [P, 2, PACK, P], F32, tag="w1_raw0")
         for u in range(2, BLK):
             sine_scalar(cos2[u], a2[u][:].rearrange("p (m t) -> p t m", t=PACK), 1, frac2[:, u - 2])
 
@@ -227,36 +223,40 @@ def tile_list_tapping_panel_ledger_kernel(
             for u in range(BLK):
                 nc.tensor.matmul(
                     total[:, u * P : (u + 1) * P], lhsT=cos2[u][:, t, :], rhs=ident[:],
-                    start=(u == 0), stop=False, is_transpose=True,
+                    start=(u == 0), stop=(t == 0 and u == BLK - 1), is_transpose=True,
                 )
+            h.append(held("h%d" % t, [P, S], F32))
             sin1 = ring.tile([P, BLK, P], F32, name="sin1")
             if t == 0:
+                cos_part = held("cos_part", [P, S], F32)
+                nc.scalar.activation(cos_part[:], total[:], ACT.Copy, scale=gain_t[:, 0:1])
                 rem0 = held("rem0", [P, BLK, P], F32, tag="frac1")
                 sine_vector(sin1[:], a1[0][:].rearrange("p (u m) -> p u m", u=BLK), 0, rem0)
-            else:
-                frac1 = held("frac1_%d" % t, [P, S], F32, tag="frac1")
-                nc.scalar.activation(frac1[:], a1[t][:], ACT.Copy, scale=1.0 / TWO_PI)
-                turns1 = ring.tile([P, S], U32, name="turns1")
-                nc.scalar.activation(turns1[:], frac1[:], ACT.Copy, bias=ROUNDER)
-                back1 = ring.tile([P, S], F32, name="back1")
-                nc.scalar.activation(back1[:], turns1[:], ACT.Copy, scale=-1.0, bias=ROUNDER)
-                rem1 = bank(4 + t, "rem1_%d" % t)
-                for i, part in enumerate((frac1, back1)):
-                    for u in range(BLK):
-                        nc.tensor.matmul(
-                            rem1[:, u * P : (u + 1) * P], lhsT=part[:, u * P : (u + 1) * P], rhs=ident[:],
-                            start=(i == 0 and u == 0), stop=(i == 1 and u == BLK - 1), is_transpose=True,
-                        )
-                nc.scalar.activation(
-                    sin1[:], rem1[:].rearrange("p (u m) -> p u m", u=BLK), ACT.Sin, scale=TWO_PI
+                nc.vector.scalar_tensor_tensor(
+                    h[0][:], sin1[:].rearrange("p u m -> p (u m)"), gain_t[:, 0:1], cos_part[:], ALU.mult, ALU.add
                 )
+                continue
+            frac1 = held("frac1_%d" % t, [P, S], F32, tag="cos_part" if t == 2 else "frac1")
+            nc.scalar.activation(frac1[:], a1[t][:], ACT.Copy, scale=1.0 / TWO_PI)
+            turns1 = ring.tile([P, S], U32, name="turns1")
+            nc.scalar.activation(turns1[:], frac1[:], ACT.Copy, bias=ROUNDER)
+            back1 = held("back1_%d" % t, [P, S], F32, tag="back1_%d" % (t % 2))
+            nc.scalar.activation(back1[:], turns1[:], ACT.Copy, scale=-1.0, bias=ROUNDER)
+            rem1 = bank(4 + t, "rem1_%d" % t)
+            for i, part in enumerate((frac1, back1)):
+                for u in range(BLK):
+                    nc.tensor.matmul(
+                        rem1[:, u * P : (u + 1) * P], lhsT=part[:, u * P : (u + 1) * P], rhs=ident[:],
+                        start=(i == 0 and u == 0), stop=(i == 1 and u == BLK - 1), is_transpose=True,
+                    )
+            nc.scalar.activation(sin1[:], rem1[:].rearrange("p (u m) -> p u m", u=BLK), ACT.Sin, scale=TWO_PI)
             for u in range(BLK):
                 nc.tensor.matmul(
                     total[:, u * P : (u + 1) * P], lhsT=sin1[:, u, :], rhs=ident[:],
                     start=False, stop=(u == BLK - 1), is_transpose=True,
                 )
-            h.append(held("h%d" % t, [P, S], F32))
             nc.scalar.activation(h[t][:], total[:], ACT.Copy, scale=gain_t[:, t : t + 1])
+
         w4_w = held("w4_w", [P, H], I32)
         nc.vector.tensor_copy(
             w4_w[:].rearrange("p (t m) -> p m t", t=PACK), w4_w_raw[:].rearrange("p (m t) -> p m t", t=PACK)
@@ -266,7 +266,7 @@ def tile_list_tapping_panel_ledger_kernel(
             w4_s[:].rearrange("p (t m) -> p m t", t=PACK), w4_s_raw[:].rearrange("p (m t) -> p m t", t=PACK)
         )
 
-        w3_bf = held("w3_bf", [P, PACK * H], BF16)
+        w3_bf = held("w3_bf", [P, PACK * H], BF16, tag="back1_1")
         deal_and_round(nc.scalar.copy, w3_bf, w3_raw, 0)
 
 
@@ -282,7 +282,7 @@ def tile_list_tapping_panel_ledger_kernel(
             nc.scalar.activation(other[:, t, :], rested[t][:], ACT.Copy, scale=rest_t[:, t : t + 1])
 
         for t in range(PACK):
-            nc.vector.tensor_tensor(page[t][:].indirect(idx2[:]), h[t][:], wgs_t[:, t * S : (t + 1) * S], ALU.mult)
+            nc.vector.tensor_tensor(page[t][:].indirect(idx2[:]), h[t][:], wgs_t[t], ALU.mult)
             due = held("due%d" % t, [P, S], F32)
             pieces = 1 if t < PACK - 1 else 2
             width = S // pieces
@@ -307,6 +307,7 @@ def tile_list_tapping_panel_ledger_kernel(
             if t < 2:
                 gather_rested(t, None)
                 scale_rested(t)
+
 
         gather_rested(3, None)
 
@@ -337,7 +338,7 @@ def tile_list_tapping_panel_ledger_kernel(
         for q in range(BLK):
             th = ring.tile([P, S], F32, name="th")
             nc.scalar.activation(th[:], b[q][:], ACT.Tanh)
-            z_rows = ring.tile([P, S], BF16, name="z_rows")
+            z_rows = held("z_rows%d" % q, [P, S], BF16)
             for t in range(PACK):
                 cols = slice(t * P, (t + 1) * P)
                 nc.scalar.activation(z_rows[:, cols], th[:, cols], ACT.Copy, scale=gt_t[:, t : t + 1])
@@ -371,6 +372,10 @@ def tile_list_tapping_panel_ledger_kernel(
             nc.vector.tensor_tensor(
                 best[:], y[q][:].rearrange("p (t j) -> p t j", t=PACK), other[:, :, q * P : (q + 1) * P], ALU.max
             )
-            res = held("res%d" % q, [P, PACK, P], F32)
-            nc.vector.tensor_tensor(res[:], best[:], b[q][:].rearrange("p (t j) -> p t j", t=PACK), ALU.subtract)
-            nc.sync.dma_start(out=out_rows[:, :, q * P : (q + 1) * P], in_=res[:])
+            b_rows = b[q][:].rearrange("p (t j) -> p t j", t=PACK)
+            step = PACK if q < BLK - 1 else PACK // 2
+            for t0 in range(0, PACK, step):
+                rows = slice(t0, t0 + step)
+                res = held("res%d_%d" % (q, t0), [P, step, P], F32)
+                nc.vector.tensor_tensor(res[:], best[:, rows], b_rows[:, rows], ALU.subtract)
+                nc.sync.dma_start(out=out_rows[:, rows, q * P : (q + 1) * P], in_=res[:])

import math
from contextlib import ExitStack

import concourse.mybir as mybir
from concourse.masks import make_identity

K, H, T, S, T2 = 1536, 512, 2048, 512, 1024
FLOPS = 2 * (2 * K * H * S + 2 * H * H * S)

F32 = mybir.dt.float32
BF16 = mybir.dt.bfloat16
I32 = mybir.dt.int32
U32 = mybir.dt.uint32
U16 = mybir.dt.uint16
U8 = mybir.dt.uint8
FP8X4 = mybir.dt.float8_e4m3fn_x4
FP4X4 = mybir.dt.float4_e2m1fn_x4
ALU = mybir.AluOpType
ACT = mybir.ActivationFunctionType

P = 128
PACK = 4
PASSES = K // (P * PACK)
QUADS = 4
BLK = S // P
TWO_PI = 2.0 * math.pi
ROUNDER = 1.5 * 2.0**23


def tile_list_tapping_panel_ledger_kernel(
    tc, tab_words, tab_scales, offs, offs2, offs3, offs4, w1, w2_words, w2_scales, gain, wgs, page0, sx, w3, gt,
    w4_words, w4_scales, rest, out,
):
    nc = tc.nc
    with ExitStack() as ctx:
        lists = ctx.enter_context(tc.tile_pool(name="lists", bufs=1))
        keep = ctx.enter_context(tc.tile_pool(name="keep", bufs=1))
        ring = ctx.enter_context(tc.tile_pool(name="ring", bufs=2))
        psum = ctx.enter_context(tc.psum_pool(name="psum", bufs=1))

        def held(name, shape, dtype, tag=None):
            return keep.tile(shape, dtype, name=name, tag=tag or name, align_bytes=64)

        def bank(number, name):
            return psum.tile([P, S], F32, name=name, tag="bank%d" % number)

        tab_s = held("tab_s", [P, PASSES * T], U8)
        w2_s = held("w2_s", [P, PASSES * H], U8)
        w4_s_raw = held("w4_s_raw", [P, H], U8)
        nc.vector.memset(tab_s[:].bitcast(I32), 0)
        nc.gpsimd.memset(w2_s[:].bitcast(I32), 0)
        nc.gpsimd.memset(w4_s_raw[:].bitcast(I32), 0)
        warm_in = held("warm_in", [P, 8], F32)
        warm_out = held("warm_out", [P, 8], F32)
        nc.gpsimd.memset(warm_in[:], 0.0)
        nc.scalar.activation(warm_out[:], warm_in[:], ACT.Silu)
        ident = held("ident", [P, P], F32)
        make_identity(nc, ident[:])

        def load_list(name, src):
            tile = lists.tile([P, S // 16], U16, name=name, tag=name)
            nc.sync.dma_start(tile[:], src)
            return tile

        def load_scale_rows(plane, src):
            passes = src.shape[0]
            for r in range(4):
                nc.sync.dma_start(
                    out=plane[r:P:32, :].bitcast(I32).rearrange("q (a n) -> q a n", a=passes),
                    in_=src[:, r:16:4, :].bitcast(I32).rearrange("a q n -> q a n"),
                )

        def load_tab(a):
            tile = held("tab_w%d" % a, [P, T], I32)
            nc.sync.dma_start(out=tile[:], in_=tab_words[a].rearrange("p n i -> p (n i)").bitcast(I32))
            return tile

        def load_rows(name, src):
            tile = held(name, [P, PACK, src.shape[1]], F32)
            nc.sync.dma_start(out=tile[:], in_=src.rearrange("(p j) c -> p j c", j=PACK))
            return tile

        def load_vector(name, src):
            tile = held(name, [P, PACK], F32)
            nc.sync.dma_start(out=tile[:], in_=src.rearrange("(p t) -> p t", t=PACK))
            return tile

        def load_wgs(name, t0, t1):
            tile = held(name, [P, (t1 - t0) * S], F32)
            rows = wgs.rearrange("(p t) j -> p (t j)", t=PACK)[:, t0 * S : t1 * S]
            for q in (0, 2, 1, 3):
                nc.sync.dma_start(out=tile[32 * q : 32 * (q + 1), :], in_=rows)
            return tile

        def load_page(t):
            tile = held("page%d" % t, [P, T2], F32)
            nc.sync.dma_start(out=tile[:], in_=page0.rearrange("(p t) c -> t p c", t=PACK)[t])
            return tile

        idx = load_list("idx", offs)
        tab_w = [load_tab(0)]
        load_scale_rows(tab_s, tab_scales)
        tab_w.append(load_tab(1))
        w2_w = held("w2_w", [P, PASSES * 2 * H], U8)
        nc.sync.dma_start(
            out=w2_w[:].bitcast(I32).rearrange("p (a n) -> p a n", a=PASSES),
            in_=w2_words.bitcast(I32).rearrange("a p n -> p a n"),
        )
        load_scale_rows(w2_s, w2_scales)
        tab_w.append(load_tab(2))
        w1_raw = [load_rows("w1_raw0", w1[0:512, :])]
        w1_raw.append(load_rows("w1_raw1", w1[512:1024, :]))
        w1_last = [load_rows("w1_last%d" % c, w1[1024:1536, 256 * c : 256 * (c + 1)]) for c in range(2)]
        gain_t = load_vector("gain_t", gain)
        idx2 = load_list("idx2", offs2)
        page = [load_page(0)]
        wgs_first = load_wgs("wgs_first", 0, 1)
        w4_w_raw = held("w4_w_raw", [P, H], I32)
        nc.sync.dma_start(out=w4_w_raw[:], in_=w4_words[0].rearrange("p n i -> p (n i)").bitcast(I32))
        load_scale_rows(w4_s_raw, w4_scales)
        wgs_later = load_wgs("wgs_later", 1, PACK)
        wgs_t = [wgs_first[:]] + [wgs_later[:, i * S : (i + 1) * S] for i in range(PACK - 1)]
        sx_t = load_vector("sx_t", sx)
        idx3 = load_list("idx3", offs3)
        page.append(load_page(1))
        w3_raw = load_rows("w3_raw", w3)
        idx4 = load_list("idx4", offs4)
        rest_t = load_vector("rest_t", rest)
        gt_t = load_vector("gt_t", gt)
        page.append(load_page(2))
        page.append(load_page(3))

        v_w, v_s = [], []
        for a in range(PASSES):
            words = held("v_w%d" % a, [P, S], U32)
            nc.vector.tensor_copy(words[:], tab_w[a][:].bitcast(U32).indirect(idx[:]))
            v_w.append(words)
            scales = held("v_s%d" % a, [P, S], U8)
            nc.vector.tensor_copy(scales[:], tab_s[:, a * T : (a + 1) * T].indirect(idx[:]))
            v_s.append(scales)

        a2 = [bank(u, "a2_%d" % u) for u in range(BLK)]
        for a in range(PASSES):
            for u in range(BLK):
                toks = slice(u * P, (u + 1) * P)
                nc.tensor.matmul_mx(
                    out=a2[u][:],
                    lhsT=v_w[a][:, toks].bitcast(FP8X4),
                    lhsT_scale=v_s[a][:, toks],
                    rhs=w2_w[:, a * 2 * H : (a + 1) * 2 * H].bitcast(FP4X4),
                    rhs_scale=w2_s[:, a * H : (a + 1) * H],
                    start=(a == 0),
                    stop=(a == PASSES - 1),
                )
        def sine_vector(result, acc, quarter_turns, rem):
            turns = ring.tile([P, PACK, P], I32, name="turns_v")
            nc.vector.tensor_scalar(turns[:], acc, 1.0 / TWO_PI, 0.25 * quarter_turns, ALU.mult, ALU.add)
            nc.vector.scalar_tensor_tensor(rem[:], turns[:], -TWO_PI, acc, ALU.mult, ALU.add)
            nc.scalar.activation(result, rem[:], ACT.Sin, bias=quarter_turns * math.pi / 2)

        def sine_scalar(result, acc, quarter_turns, frac):
            nc.scalar.activation(frac, acc, ACT.Copy, scale=1.0 / TWO_PI, bias=0.25 * quarter_turns)
            turns = ring.tile([P, PACK, P], U32, name="turns_s")
            nc.scalar.activation(turns[:], frac, ACT.Copy, bias=ROUNDER)
            rem = ring.tile([P, PACK, P], F32, name="rem", bufs=BLK)
            nc.vector.scalar_tensor_tensor(
                rem[:], turns[:].bitcast(I32), ROUNDER, frac, ALU.subtract, ALU.subtract
            )
            nc.scalar.activation(result, rem[:], ACT.Sin, scale=-TWO_PI)

        cos_all = held("cos_all", [P, BLK, PACK, P], F32, tag="w1_last0")
        cos2 = [cos_all[:, u] for u in range(BLK)]
        for u in range(2):
            rem2 = ring.tile([P, PACK, P], F32, name="rem", bufs=BLK)
            sine_vector(cos2[u], a2[u][:].rearrange("p (m t) -> p t m", t=PACK), 1, rem2)

        def deal_and_round(copy, grouped, raw, m0):
            count = raw.shape[2] // PACK
            copy(
                grouped[:].rearrange("p (t m j) -> p m j t", t=PACK, j=PACK)[:, m0 : m0 + count],
                raw[:].rearrange("p j (m t) -> p m j t", t=PACK),
            )

        def quantise(codes, scales, grouped, c0, count):
            nc.vector.quantize_mx(
                out=codes[:, c0 : c0 + count].bitcast(FP8X4),
                scales=scales[:, c0 : c0 + count],
                in_=grouped[:, PACK * c0 : PACK * (c0 + count)],
            )

        w1_w = [held("w1_w%d" % a, [P, H], U32) for a in range(PASSES)]
        w1_s = [held("w1_s%d" % a, [P, H], U8) for a in range(PASSES)]
        for a in range(PASSES - 1):
            grouped = held("w1_bf%d" % a, [P, PACK * H], BF16)
            deal_and_round(nc.scalar.copy if a == 0 else nc.vector.tensor_copy, grouped, w1_raw[a], 0)
            quantise(w1_w[a], w1_s[a], grouped, 0, H)
        grouped = held("w1_bf2", [P, PACK * H], BF16)
        for c in range(2):
            deal_and_round(nc.scalar.copy if c == 0 else nc.vector.tensor_copy, grouped, w1_last[c], 64 * c)
        for t in range(PACK):
            quantise(w1_w[2], w1_s[2], grouped, t * P, P)

        a1 = [bank(4 + t, "a1_%d" % t) for t in range(PACK)]
        for a in range(PASSES):
            for t in range(PACK):
                nc.tensor.matmul_mx(
                    out=a1[t][:],
                    lhsT=w1_w[a][:, t * P : (t + 1) * P].bitcast(FP8X4),
                    lhsT_scale=w1_s[a][:, t * P : (t + 1) * P],
                    rhs=v_w[a][:].bitcast(FP8X4),
                    rhs_scale=v_s[a][:],
                    start=(a == 0),
                    stop=(a == PASSES - 1),
                )

        frac2 = held("frac2", [P, 2, PACK, P], F32, tag="w1_raw0")
        for u in range(2, BLK):
            sine_scalar(cos2[u], a2[u][:].rearrange("p (m t) -> p t m", t=PACK), 1, frac2[:, u - 2])

        h = []
        for t in range(PACK):
            total = bank(t, "total%d" % t)
            for u in range(BLK):
                nc.tensor.matmul(
                    total[:, u * P : (u + 1) * P], lhsT=cos2[u][:, t, :], rhs=ident[:],
                    start=(u == 0), stop=(t == 0 and u == BLK - 1), is_transpose=True,
                )
            h.append(held("h%d" % t, [P, S], F32))
            sin1 = ring.tile([P, BLK, P], F32, name="sin1")
            if t == 0:
                cos_part = held("cos_part", [P, S], F32)
                nc.scalar.activation(cos_part[:], total[:], ACT.Copy, scale=gain_t[:, 0:1])
                rem0 = held("rem0", [P, BLK, P], F32, tag="frac1")
                sine_vector(sin1[:], a1[0][:].rearrange("p (u m) -> p u m", u=BLK), 0, rem0)
                nc.vector.scalar_tensor_tensor(
                    h[0][:], sin1[:].rearrange("p u m -> p (u m)"), gain_t[:, 0:1], cos_part[:], ALU.mult, ALU.add
                )
                continue
            frac1 = held("frac1_%d" % t, [P, S], F32, tag="cos_part" if t == 2 else "frac1")
            nc.scalar.activation(frac1[:], a1[t][:], ACT.Copy, scale=1.0 / TWO_PI)
            turns1 = ring.tile([P, S], U32, name="turns1")
            nc.scalar.activation(turns1[:], frac1[:], ACT.Copy, bias=ROUNDER)
            back1 = held("back1_%d" % t, [P, S], F32, tag="back1_%d" % (t % 2))
            nc.scalar.activation(back1[:], turns1[:], ACT.Copy, scale=-1.0, bias=ROUNDER)
            rem1 = bank(4 + t, "rem1_%d" % t)
            for i, part in enumerate((frac1, back1)):
                for u in range(BLK):
                    nc.tensor.matmul(
                        rem1[:, u * P : (u + 1) * P], lhsT=part[:, u * P : (u + 1) * P], rhs=ident[:],
                        start=(i == 0 and u == 0), stop=(i == 1 and u == BLK - 1), is_transpose=True,
                    )
            nc.scalar.activation(sin1[:], rem1[:].rearrange("p (u m) -> p u m", u=BLK), ACT.Sin, scale=TWO_PI)
            for u in range(BLK):
                nc.tensor.matmul(
                    total[:, u * P : (u + 1) * P], lhsT=sin1[:, u, :], rhs=ident[:],
                    start=False, stop=(u == BLK - 1), is_transpose=True,
                )
            nc.scalar.activation(h[t][:], total[:], ACT.Copy, scale=gain_t[:, t : t + 1])

        w4_w = held("w4_w", [P, H], I32)
        nc.vector.tensor_copy(
            w4_w[:].rearrange("p (t m) -> p m t", t=PACK), w4_w_raw[:].rearrange("p (m t) -> p m t", t=PACK)
        )
        w4_s = held("w4_s", [P, H], U8)
        nc.vector.tensor_copy(
            w4_s[:].rearrange("p (t m) -> p m t", t=PACK), w4_s_raw[:].rearrange("p (m t) -> p m t", t=PACK)
        )

        w3_bf = held("w3_bf", [P, PACK * H], BF16, tag="back1_1")
        deal_and_round(nc.scalar.copy, w3_bf, w3_raw, 0)


        x_bf = [held("x_bf%d" % c, [P, 256 * PACK], BF16) for c in range(2)]
        other = held("other", [P, PACK, S], F32)
        rested = {}

        def gather_rested(t, tag):
            rested[t] = held("rested%d" % t, [P, S], F32, tag=tag)
            nc.vector.tensor_copy(rested[t][:], page[t][:].indirect(idx4[:]))

        def scale_rested(t):
            nc.scalar.activation(other[:, t, :], rested[t][:], ACT.Copy, scale=rest_t[:, t : t + 1])

        for t in range(PACK):
            nc.vector.tensor_tensor(page[t][:].indirect(idx2[:]), h[t][:], wgs_t[t], ALU.mult)
            due = held("due%d" % t, [P, S], F32)
            pieces = 1 if t < PACK - 1 else 2
            width = S // pieces
            for c in range(pieces):
                nc.vector.tensor_copy(
                    due[:, c * width : (c + 1) * width],
                    page[t][:].indirect(idx3[:, c * width // 16 : (c + 1) * width // 16]),
                )
            width = 256 if t < PACK - 1 else P
            for c0 in range(0, S, width):
                lanes = x_bf[c0 // 256][:].rearrange("p (j t) -> p t j", t=PACK)
                nc.scalar.activation(
                    lanes[:, t, c0 % 256 : c0 % 256 + width],
                    due[:, c0 : c0 + width],
                    ACT.Copy,
                    scale=sx_t[:, t : t + 1],
                )
            if t == 2:
                w3_w = held("w3_w", [P, H], U32, tag="h2")
                w3_s = held("w3_s", [P, H], U8)
                quantise(w3_w, w3_s, w3_bf, 0, H)
            if t < 2:
                gather_rested(t, None)
                scale_rested(t)


        gather_rested(3, None)

        b = []
        for q in range(BLK):
            x_w = held("x_w%d" % q, [P, P], U32)
            x_s = held("x_s%d" % q, [P, P], U8)
            c0 = (q % 2) * P * PACK
            nc.vector.quantize_mx(
                out=x_w[:].bitcast(FP8X4), scales=x_s[:], in_=x_bf[q // 2][:, c0 : c0 + P * PACK]
            )
            acc = bank(4 + q, "b%d" % q)
            for t in range(PACK):
                cols = slice(t * P, (t + 1) * P)
                nc.tensor.matmul_mx(
                    out=acc[:, cols],
                    lhsT=w3_w[:, cols].bitcast(FP8X4),
                    lhsT_scale=w3_s[:, cols],
                    rhs=x_w[:].bitcast(FP8X4),
                    rhs_scale=x_s[:],
                    start=True,
                    stop=True,
                )
            b.append(acc)
        gather_rested(2, "x_bf1")

        y = []
        for q in range(BLK):
            th = ring.tile([P, S], F32, name="th")
            nc.scalar.activation(th[:], b[q][:], ACT.Tanh)
            z_rows = held("z_rows%d" % q, [P, S], BF16)
            for t in range(PACK):
                cols = slice(t * P, (t + 1) * P)
                nc.scalar.activation(z_rows[:, cols], th[:, cols], ACT.Copy, scale=gt_t[:, t : t + 1])
            z_bf = ring.tile([P, S], BF16, name="z_bf", align_bytes=64)
            nc.vector.tensor_copy(
                z_bf[:].rearrange("p (c i t) -> p c t i", i=4, t=PACK),
                z_rows[:].rearrange("p (t c i) -> p c t i", i=4, t=PACK),
            )
            z_w = ring.tile([P, P], U32, name="z_w", align_bytes=64)
            z_s = ring.tile([P, P], U8, name="z_s", align_bytes=64)
            nc.vector.quantize_mx(out=z_w[:].bitcast(FP8X4), scales=z_s[:], in_=z_bf[:])
            acc = bank(q, "y%d" % q)
            for t in range(PACK):
                cols = slice(t * P, (t + 1) * P)
                nc.tensor.matmul_mx(
                    out=acc[:, cols],
                    lhsT=w4_w[:, cols].bitcast(FP8X4),
                    lhsT_scale=w4_s[:, cols],
                    rhs=z_w[:].bitcast(FP8X4),
                    rhs_scale=z_s[:],
                    start=True,
                    stop=True,
                )
            y.append(acc)
            if q < 2:
                scale_rested(3 - q)

        out_rows = out.rearrange("(p t) j -> p t j", t=PACK)
        for q in range(BLK):
            best = ring.tile([P, PACK, P], F32, name="best")
            nc.vector.tensor_tensor(
                best[:], y[q][:].rearrange("p (t j) -> p t j", t=PACK), other[:, :, q * P : (q + 1) * P], ALU.max
            )
            b_rows = b[q][:].rearrange("p (t j) -> p t j", t=PACK)
            step = PACK if q < BLK - 1 else PACK // 2
            for t0 in range(0, PACK, step):
                rows = slice(t0, t0 + step)
                res = held("res%d_%d" % (q, t0), [P, step, P], F32)
                nc.vector.tensor_tensor(res[:], best[:, rows], b_rows[:, rows], ALU.subtract)
                nc.sync.dma_start(out=out_rows[:, rows, q * P : (q + 1) * P], in_=res[:])
